import numpy as np
import ml_dtypes


def mxq(x, axis, fmt="e4m3"):
    dtype, down = {"e4m3": (ml_dtypes.float8_e4m3fn, 7), "e5m2": (ml_dtypes.float8_e5m2, 14)}[fmt]
    v = np.moveaxis(np.asarray(x, np.float32).astype(ml_dtypes.bfloat16).astype(np.float64), axis, -1)
    blocks = v.reshape(v.shape[:-1] + (-1, 32))
    amax = np.abs(blocks).max(-1, keepdims=True)
    byte = np.maximum(np.where(amax > 0, np.frexp(amax)[1] - 1 + 127, 0) - down, 1)
    scale = np.exp2(byte - 127.0)
    codes = (blocks / scale).astype(np.float32).astype(dtype).astype(np.float64)
    return np.moveaxis((codes * scale).reshape(v.shape), -1, axis)


WIDE = False


def mx_kscale(k):
    if not WIDE:
        return np.ones(k)
    levels = np.array([10, -10, 5, -5, 0])
    if k % 512:
        return np.exp2(np.random.permutation(np.resize(levels, k // 32))).repeat(32)
    a = np.empty((k // 512, 16))
    for p in range(k // 512):
        a[p, :8] = np.random.permutation(np.resize(levels, 8))
        for g in range(8):
            far = levels[np.abs(levels - a[p, g]) >= 10]
            a[p, g + 8] = far[np.random.randint(len(far))]
    return np.exp2(a.ravel()).repeat(32)


def f64(x):
    return np.asarray(x).astype(np.float64)


def striped(idx):
    return np.tile(idx.reshape(-1, 16).T, (8, 1)).astype(np.uint16)


def unstriped(offs):
    return offs[:16].T.reshape(-1).astype(np.int64)


E2M1 = np.array([0.0, 0.5, 1.0, 1.5, 2.0, 3.0, 4.0, 6.0, -0.0, -0.5, -1.0, -1.5, -2.0, -3.0, -4.0, -6.0])


def pack_weight(w, fmt):
    k, n = w.shape
    w = f64(np.asarray(w, np.float32).astype(ml_dtypes.bfloat16)).reshape(k // 32, 32, n)
    amax = np.abs(w).max(1)
    if fmt == "e4m3":
        byte = np.frexp(amax)[1] - 1 + 127 - 7
    else:
        mant, ex = np.frexp(amax / 6.0)
        byte = np.where(mant > 0.5, ex, ex - 1) + 127
    byte = np.clip(np.where(amax > 0, byte, 1), 1, 254)
    scaled = (w * np.exp2(127.0 - byte)[:, None, :]).reshape(k, n).astype(np.float32)
    by_word = np.ascontiguousarray(scaled.reshape(k // 512, 128, 4, n).transpose(0, 1, 3, 2))
    if fmt == "e4m3":
        words = by_word.astype(ml_dtypes.float8_e4m3fn).view(np.uint8)
    else:
        c = by_word.astype(ml_dtypes.float4_e2m1fn).view(np.uint8) & 0xF
        words = (c[..., 0::2] | (c[..., 1::2] << 4)).reshape(k // 512, 128, 2 * n)
    return np.ascontiguousarray(words), np.ascontiguousarray(byte.astype(np.uint8).reshape(k // 512, 16, n))


def unpack_weight(words, scales, fmt):
    g, _, n = scales.shape
    words = np.ascontiguousarray(words).reshape(g, 128, n, -1)
    if fmt == "e4m3":
        vals = words.view(ml_dtypes.float8_e4m3fn).astype(np.float64)
    else:
        nib = np.empty((g, 128, n, 4), np.uint8)
        nib[..., 0::2] = words & 0xF
        nib[..., 1::2] = words >> 4
        vals = E2M1[nib]
    vals = vals * np.repeat(np.exp2(scales.astype(np.float64) - 127.0), 8, axis=1)[..., None]
    return vals.transpose(0, 1, 3, 2).reshape(g * 512, n)


def relu(v):
    return np.maximum(v, 0.0)


K, T, E, H, N = 512, 768, 4, 512, 384
COUNTS = (256, 384, 512, 384)
STARTS = np.cumsum((0,) + COUNTS)


def by_expert(wq, xq):
    return np.concatenate([wq[e].T @ xq[:, STARTS[e]:STARTS[e + 1]] for e in range(E)], axis=1)


def setup_inputs():
    n = np.random.standard_normal
    s = mx_kscale(K)[:, None]
    u = mx_kscale(H)
    both = np.repeat(np.arange(E), COUNTS)
    pair = np.stack([both[:T], both[T:]])[:, np.random.permutation(T)]
    pair = np.where(np.random.rand(T) < 0.5, pair, pair[::-1])
    order = np.argsort(pair.reshape(-1), kind="stable")
    slot_token = order % T; pos = np.empty(2 * T, np.int64); pos[order] = np.arange(2 * T); pos = pos.reshape(2, T)
    g = np.random.uniform(0.2, 0.8, T)
    w1 = [pack_weight(m, "e2m1") for m in n((E, K, H)) / np.sqrt(K) / s[None] * u[None, None, :]]
    w2 = [pack_weight(m, "e2m1") for m in n((E, H, N)) / np.sqrt(H) / u[None, :, None]]
    return {
        "xT": (n((K, T)) * s).astype(np.float32),
        "w1_words": np.stack([m[0] for m in w1]),
        "w1_scales": np.stack([m[1] for m in w1]),
        "w2_words": np.stack([m[0] for m in w2]),
        "w2_scales": np.stack([m[1] for m in w2]),
        "gate": np.stack([np.tile(g, (N, 1)), np.tile(1.0 - g, (N, 1))]).astype(np.float32),
        "offs": striped(slot_token),
        "pos1": striped(pos[0]),
        "pos2": striped(pos[1]),
    }


def reference(xT, w1_words, w1_scales, w2_words, w2_scales, gate, offs, pos1, pos2):
    idx = unstriped(offs)
    w1 = np.stack([unpack_weight(w1_words[e], w1_scales[e], "e2m1") for e in range(E)])
    w2 = np.stack([unpack_weight(w2_words[e], w2_scales[e], "e2m1") for e in range(E)])
    xq = mxq(f64(xT)[:, idx], 0, "e4m3")
    h = relu(by_expert(w1, xq))
    y = by_expert(w2, mxq(h, 0, "e4m3"))
    return f64(gate[0]) * y[:, unstriped(pos1)] + f64(gate[1]) * y[:, unstriped(pos2)]

@@ -1,0 +1,237 @@
+from contextlib import ExitStack
+
+import concourse.mybir as mybir
+
+K, T, E, H, N = 512, 768, 4, 512, 384
+COUNTS = (256, 384, 512, 384)
+STARTS = (0, 256, 640, 1152)
+S = 1536
+P = 128
+PACK = 4
+CH = 128
+XC = 256
+FLOPS = 2 * S * (K * H + H * N)
+
+F32 = mybir.dt.float32
+BF16 = mybir.dt.bfloat16
+I32 = mybir.dt.int32
+U32 = mybir.dt.uint32
+U16 = mybir.dt.uint16
+U8 = mybir.dt.uint8
+FP8X4 = mybir.dt.float8_e4m3fn_x4
+FP4X4 = mybir.dt.float4_e2m1fn_x4
+COPY = mybir.ActivationFunctionType.Copy
+RELU = mybir.ActivationFunctionType.Relu
+MULT = mybir.AluOpType.mult
+ADD = mybir.AluOpType.add
+
+
+def tile_moe_rag_mlp_relu_kernel(
+    tc, xT, w1_words, w1_scales, w2_words, w2_scales, gate, offs, pos1, pos2, out
+):
+    nc = tc.nc
+    with ExitStack() as ctx:
+        lists = ctx.enter_context(tc.tile_pool(name="lists", bufs=1))
+        keep = ctx.enter_context(tc.tile_pool(name="keep", bufs=1))
+        ring = ctx.enter_context(tc.tile_pool(name="ring", bufs=3))
+        psum = ctx.enter_context(tc.psum_pool(name="psum", bufs=1))
+
+        offs_t = lists.tile([P, 2 * T // 16], U16, name="offs_t")
+        pos1_t = lists.tile([P, T // 16], U16, name="pos1_t")
+        pos2_t = lists.tile([P, T // 16], U16, name="pos2_t")
+
+        w1_raw = [keep.tile([P, 2, 2 * H], U8, name=f"w1_raw{i}", align_bytes=64) for i in range(2)]
+        w1_codes = [keep.tile([P, 2, 2 * H], U8, name=f"w1_codes{i}", align_bytes=64) for i in range(2)]
+        w1s_raw = keep.tile([P, E, H], U8, name="w1s_raw", align_bytes=64)
+        w1s = [keep.tile([P, 2, H], U8, name=f"w1s{i}", align_bytes=64) for i in range(2)]
+        w2_codes = keep.tile([P, E, 2 * N], U8, name="w2_codes", align_bytes=64)
+        w2s = keep.tile([P, E, N], U8, name="w2s", align_bytes=64)
+        x_raw = [keep.tile([P, PACK, XC], F32, name=f"x_raw{c}", align_bytes=64) for c in range(3)]
+        x_grp = [keep.tile([P, XC, PACK], BF16, name=f"x_grp{c}", align_bytes=64) for c in range(3)]
+        x_codes = keep.tile([P, T], U32, name="x_codes", align_bytes=64)
+        x_scales = keep.tile([P, T], U8, name="x_scales", align_bytes=64)
+        gates = [keep.tile([P, 2, T], F32, name=f"gates{b}", align_bytes=64) for b in range(3)]
+        ys = [keep.tile([P, S], F32, name=f"y{b}", align_bytes=64) for b in range(3)]
+
+        nc.vector.memset(w1s_raw[:].rearrange("p e n -> p (e n)").bitcast(I32), 0)
+        nc.vector.memset(w2s[:].rearrange("p e n -> p (e n)").bitcast(I32), 0)
+        nc.gpsimd.memset(x_scales[:], 0)
+
+        def load_x(c):
+            nc.sync.dma_start(out=x_raw[c][:], in_=xT[:, c * XC : (c + 1) * XC].rearrange("(p j) w -> p j w", j=PACK))
+
+        def load_w1(i):
+            nc.sync.dma_start(
+                out=w1_raw[i][:].bitcast(I32),
+                in_=w1_words[2 * i : 2 * i + 2, 0].rearrange("e p b -> p e b").bitcast(I32),
+            )
+
+        for q in range(4):
+            nc.scalar.dma_start(
+                out=w1s_raw[32 * q : 32 * q + 4].bitcast(I32),
+                in_=w1_scales[:, 0, 4 * q : 4 * q + 4, :].rearrange("e q n -> q e n").bitcast(I32),
+            )
+        for q in range(4):
+            nc.gpsimd.dma_start(
+                out=w2s[32 * q : 32 * q + 4].bitcast(I32),
+                in_=w2_scales[:, 0, 4 * q : 4 * q + 4, :].rearrange("e q n -> q e n").bitcast(I32),
+            )
+        load_w1(0)
+        load_x(0)
+        load_w1(1)
+        nc.sync.dma_start(offs_t[:], offs)
+        load_x(1)
+        load_x(2)
+        nc.sync.dma_start(out=w2_codes[:].bitcast(I32), in_=w2_words[:, 0].rearrange("e p b -> p e b").bitcast(I32))
+        nc.sync.dma_start(pos1_t[:], pos1)
+        nc.sync.dma_start(pos2_t[:], pos2)
+        for b in range(3):
+            nc.sync.dma_start(out=gates[b][:], in_=gate[:, b * P : (b + 1) * P, :].rearrange("g p t -> p g t"))
+
+        def x_quant(c):
+            nc.vector.quantize_mx(
+                out=x_codes[:, c * XC : (c + 1) * XC].bitcast(FP8X4),
+                scales=x_scales[:, c * XC : (c + 1) * XC],
+                in_=x_grp[c][:].rearrange("p w j -> p (w j)"),
+            )
+
+        def w1_permute(i):
+            for e in range(2):
+                nc.vector.tensor_copy(
+                    out=w1_codes[i][:, e, :].bitcast(U16).rearrange("p (t m) -> p t m", t=PACK),
+                    in_=w1_raw[i][:, e, :].bitcast(U16).rearrange("p (m t) -> p t m", t=PACK),
+                )
+            for e in range(2):
+                nc.vector.tensor_copy(
+                    out=w1s[i][:, e, :].rearrange("p (t m) -> p t m", t=PACK),
+                    in_=w1s_raw[:, 2 * i + e, :].rearrange("p (m t) -> p t m", t=PACK),
+                )
+
+        def interleave(engine, c, lo, hi):
+            o = x_grp[c][:, lo:hi, :]
+            i = x_raw[c][:, :, lo:hi].rearrange("p j w -> p w j")
+            if engine == "S":
+                nc.scalar.activation(o, i, COPY)
+            else:
+                nc.vector.tensor_copy(o, i)
+
+        interleave("S", 0, 0, XC)
+        w1_permute(0)
+        x_quant(0)
+        w1_permute(1)
+        interleave("S", 1, 0, 160)
+        interleave("V", 1, 160, XC)
+        x_quant(1)
+        interleave("V", 2, 0, 160)
+        interleave("S", 2, 160, XC)
+        x_quant(2)
+
+        xg = []
+        xgs = []
+        for e in range(E):
+            cols = slice(STARTS[e] // 16, (STARTS[e] + COUNTS[e]) // 16)
+            words = keep.tile([P, COUNTS[e]], U32, name=f"xg{e}", align_bytes=64)
+            bytes_ = keep.tile([P, COUNTS[e]], U8, name=f"xgs{e}", align_bytes=64)
+            nc.vector.tensor_copy(words[:], x_codes[:].indirect(offs_t[:, cols]))
+            nc.vector.tensor_copy(bytes_[:], x_scales[:].indirect(offs_t[:, cols]))
+            xg.append(words)
+            xgs.append(bytes_)
+
+        chunks = [(e, s) for e in range(E) for s in range(0, COUNTS[e], CH)]
+        h_codes = keep.tile([P, S], U32, name="h_codes", align_bytes=64)
+        h_scales = keep.tile([P, S], U8, name="h_scales", align_bytes=64)
+        vector_chunks = ()
+
+        def layer1(c, h_grp, at):
+            e, s = chunks[c]
+            i, ee = e // 2, e % 2
+            acc = psum.tile([P, PACK, CH], F32, name="acc", bufs=5)
+            for t in range(PACK):
+                nc.tensor.matmul_mx(
+                    out=acc[:, t, :],
+                    lhsT=w1_codes[i][:, ee, 256 * t : 256 * t + 256].bitcast(FP4X4),
+                    lhsT_scale=w1s[i][:, ee, 128 * t : 128 * t + 128],
+                    rhs=xg[e][:, s : s + CH].bitcast(FP8X4),
+                    rhs_scale=xgs[e][:, s : s + CH],
+                    start=True,
+                    stop=True,
+                )
+            o = h_grp[:, at : at + CH, :]
+            a = acc[:].rearrange("p t n -> p n t")
+            if c in vector_chunks:
+                nc.vector.tensor_scalar_max(o, a, 0.0)
+            else:
+                nc.scalar.activation(o, a, RELU)
+
+        def h_quant(h_grp, lo, width):
+            nc.vector.quantize_mx(
+                out=h_codes[:, lo : lo + width].bitcast(FP8X4),
+                scales=h_scales[:, lo : lo + width],
+                in_=h_grp[:].rearrange("p n t -> p (n t)"),
+            )
+
+        def layer2(b, acc, lo, hi, base):
+            while lo < hi:
+                e = max(k for k in range(E) if STARTS[k] <= lo)
+                end = min(hi, STARTS[e] + COUNTS[e])
+                w = max(k for k in (128, 256, 512) if k <= end - lo)
+                nc.tensor.matmul_mx(
+                    out=acc[:, lo - base : lo - base + w],
+                    lhsT=w2_codes[:, e, 256 * b : 256 * b + 256].bitcast(FP4X4),
+                    lhsT_scale=w2s[:, e, 128 * b : 128 * b + 128],
+                    rhs=h_codes[:, lo : lo + w].bitcast(FP8X4),
+                    rhs_scale=h_scales[:, lo : lo + w],
+                    start=True,
+                    stop=True,
+                )
+                lo += w
+
+        groups = [(0, 1), (2, 3), (4, 5), (6, 7), (8,), (9,), (10,), (11,)]
+        y0 = None
+        for g in groups:
+            width = CH * len(g)
+            h_grp = keep.tile([P, width, PACK], BF16, name=f"h_grp{g[0]}", align_bytes=64)
+            for n, c in enumerate(g):
+                layer1(c, h_grp, n * CH)
+            lo = g[0] * CH
+            h_quant(h_grp, lo, width)
+            base = lo // 512 * 512
+            if lo == 0:
+                y0 = psum.tile([P, 3, 512], F32, name="yp", bufs=1)
+            k = base // 512
+            layer2(0, y0[:, k, :], lo, lo + width, base)
+            if g == (10,):
+                nc.scalar.activation(ys[0][:, base : base + 384], y0[:, k, 0:384], COPY)
+            elif g == (11,):
+                nc.vector.tensor_copy(ys[0][:, base + 384 : base + 512], y0[:, k, 384:512])
+            elif lo + width == base + 512:
+                nc.scalar.activation(ys[0][:, base : base + 512], y0[:, k, :], COPY)
+
+        for b in (1, 2):
+            yb = psum.tile([P, 3, 512], F32, name="yp", bufs=1)
+            for k in range(3):
+                layer2(b, yb[:, k, :], 512 * k, 512 * k + 512, 512 * k)
+                nc.scalar.activation(ys[b][:, 512 * k : 512 * k + 512], yb[:, k, :], COPY)
+
+        def mul(b, r, lo, hi):
+            g = ring.tile([P, T], F32, name=f"m{r}", align_bytes=64)
+            pos = (pos1_t, pos2_t)[r]
+            nc.vector.tensor_tensor(
+                g[:, lo:hi], ys[b][:].indirect(pos[:, lo // 16 : hi // 16]), gates[b][:, r, lo:hi], MULT
+            )
+            return g
+
+        def finish(b, m1, m2, lo, hi):
+            o = ring.tile([P, T], F32, name="o", align_bytes=64)
+            nc.vector.tensor_tensor(o[:, lo:hi], m1[:, lo:hi], m2[:, lo:hi], ADD)
+            nc.sync.dma_start(out=out[b * P : (b + 1) * P, lo:hi], in_=o[:, lo:hi])
+
+        parts = [(0, 0, T), (1, 0, T), (2, 0, 512), (2, 512, T)]
+        pending = None
+        for b, lo, hi in parts:
+            m1 = mul(b, 0, lo, hi)
+            if pending is not None:
+                finish(*pending)
+            m2 = mul(b, 1, lo, hi)
+            pending = (b, m1, m2, lo, hi)
+        finish(*pending)

@@ -40,10 +40,10 @@ def tile_moe_rag_mlp_relu_kernel(
         pos1_t = lists.tile([P, T // 16], U16, name="pos1_t")
         pos2_t = lists.tile([P, T // 16], U16, name="pos2_t")
 
-        w1_raw = [keep.tile([P, 2, 2 * H], U8, name=f"w1_raw{i}", align_bytes=64) for i in range(2)]
-        w1_codes = [keep.tile([P, 2, 2 * H], U8, name=f"w1_codes{i}", align_bytes=64) for i in range(2)]
+        w1_raw = keep.tile([P, E, 2 * H], U8, name="w1_raw", align_bytes=64)
+        w1_codes = keep.tile([P, E, 2 * H], U8, name="w1_codes", align_bytes=64)
         w1s_raw = keep.tile([P, E, H], U8, name="w1s_raw", align_bytes=64)
-        w1s = [keep.tile([P, 2, H], U8, name=f"w1s{i}", align_bytes=64) for i in range(2)]
+        w1s = keep.tile([P, E, H], U8, name="w1s", align_bytes=64)
         w2_codes = keep.tile([P, E, 2 * N], U8, name="w2_codes", align_bytes=64)
         w2s = keep.tile([P, E, N], U8, name="w2s", align_bytes=64)
         x_raw = [keep.tile([P, PACK, XC], F32, name=f"x_raw{c}", align_bytes=64) for c in range(3)]
@@ -60,29 +60,22 @@ def tile_moe_rag_mlp_relu_kernel(
         def load_x(c):
             nc.sync.dma_start(out=x_raw[c][:], in_=xT[:, c * XC : (c + 1) * XC].rearrange("(p j) w -> p j w", j=PACK))
 
-        def load_w1(i):
-            nc.sync.dma_start(
-                out=w1_raw[i][:].bitcast(I32),
-                in_=w1_words[2 * i : 2 * i + 2, 0].rearrange("e p b -> p e b").bitcast(I32),
-            )
-
         for q in range(4):
             nc.scalar.dma_start(
                 out=w1s_raw[32 * q : 32 * q + 4].bitcast(I32),
                 in_=w1_scales[:, 0, 4 * q : 4 * q + 4, :].rearrange("e q n -> q e n").bitcast(I32),
             )
+        nc.sync.dma_start(out=w1_raw[:].bitcast(I32), in_=w1_words[:, 0].rearrange("e p b -> p e b").bitcast(I32))
+        load_x(0)
+        load_x(1)
+        load_x(2)
+        nc.sync.dma_start(offs_t[:], offs)
+        nc.sync.dma_start(out=w2_codes[:].bitcast(I32), in_=w2_words[:, 0].rearrange("e p b -> p e b").bitcast(I32))
         for q in range(4):
-            nc.gpsimd.dma_start(
+            nc.sync.dma_start(
                 out=w2s[32 * q : 32 * q + 4].bitcast(I32),
                 in_=w2_scales[:, 0, 4 * q : 4 * q + 4, :].rearrange("e q n -> q e n").bitcast(I32),
             )
-        load_w1(0)
-        load_x(0)
-        load_w1(1)
-        nc.sync.dma_start(offs_t[:], offs)
-        load_x(1)
-        load_x(2)
-        nc.sync.dma_start(out=w2_codes[:].bitcast(I32), in_=w2_words[:, 0].rearrange("e p b -> p e b").bitcast(I32))
         nc.sync.dma_start(pos1_t[:], pos1)
         nc.sync.dma_start(pos2_t[:], pos2)
         for b in range(3):
@@ -95,18 +88,6 @@ def tile_moe_rag_mlp_relu_kernel(
                 in_=x_grp[c][:].rearrange("p w j -> p (w j)"),
             )
 
-        def w1_permute(i):
-            for e in range(2):
-                nc.vector.tensor_copy(
-                    out=w1_codes[i][:, e, :].bitcast(U16).rearrange("p (t m) -> p t m", t=PACK),
-                    in_=w1_raw[i][:, e, :].bitcast(U16).rearrange("p (m t) -> p t m", t=PACK),
-                )
-            for e in range(2):
-                nc.vector.tensor_copy(
-                    out=w1s[i][:, e, :].rearrange("p (t m) -> p t m", t=PACK),
-                    in_=w1s_raw[:, 2 * i + e, :].rearrange("p (m t) -> p t m", t=PACK),
-                )
-
         def interleave(engine, c, lo, hi):
             o = x_grp[c][:, lo:hi, :]
             i = x_raw[c][:, :, lo:hi].rearrange("p j w -> p w j")
@@ -115,15 +96,20 @@ def tile_moe_rag_mlp_relu_kernel(
             else:
                 nc.vector.tensor_copy(o, i)
 
+        nc.vector.tensor_copy(
+            out=w1_codes[:].bitcast(U16).rearrange("p e (t m) -> p e t m", t=PACK),
+            in_=w1_raw[:].bitcast(U16).rearrange("p e (m t) -> p e t m", t=PACK),
+        )
+        nc.vector.tensor_copy(
+            out=w1s[:].rearrange("p e (t m) -> p e t m", t=PACK),
+            in_=w1s_raw[:].rearrange("p e (m t) -> p e t m", t=PACK),
+        )
         interleave("S", 0, 0, XC)
-        w1_permute(0)
+        interleave("S", 1, 0, XC)
         x_quant(0)
-        w1_permute(1)
-        interleave("S", 1, 0, 160)
-        interleave("V", 1, 160, XC)
-        x_quant(1)
         interleave("V", 2, 0, 160)
         interleave("S", 2, 160, XC)
+        x_quant(1)
         x_quant(2)
 
         xg = []
@@ -138,19 +124,16 @@ def tile_moe_rag_mlp_relu_kernel(
             xgs.append(bytes_)
 
         chunks = [(e, s) for e in range(E) for s in range(0, COUNTS[e], CH)]
-        h_codes = keep.tile([P, S], U32, name="h_codes", align_bytes=64)
-        h_scales = keep.tile([P, S], U8, name="h_scales", align_bytes=64)
-        vector_chunks = ()
+        vector_chunks = (9, 11)
 
         def layer1(c, h_grp, at):
             e, s = chunks[c]
-            i, ee = e // 2, e % 2
             acc = psum.tile([P, PACK, CH], F32, name="acc", bufs=5)
             for t in range(PACK):
                 nc.tensor.matmul_mx(
                     out=acc[:, t, :],
-                    lhsT=w1_codes[i][:, ee, 256 * t : 256 * t + 256].bitcast(FP4X4),
-                    lhsT_scale=w1s[i][:, ee, 128 * t : 128 * t + 128],
+                    lhsT=w1_codes[:, e, 256 * t : 256 * t + 256].bitcast(FP4X4),
+                    lhsT_scale=w1s[:, e, 128 * t : 128 * t + 128],
                     rhs=xg[e][:, s : s + CH].bitcast(FP8X4),
                     rhs_scale=xgs[e][:, s : s + CH],
                     start=True,
@@ -163,55 +146,63 @@ def tile_moe_rag_mlp_relu_kernel(
             else:
                 nc.scalar.activation(o, a, RELU)
 
-        def h_quant(h_grp, lo, width):
+        groups = [(0, 1), (2, 3), (4,), (5, 6), (7,), (8,), (9,), (10,), (11,)]
+        h_grps, h_codes, h_scales = {}, {}, {}
+
+        def h_make(g):
+            h_grps[g] = keep.tile([P, CH * len(g), PACK], BF16, name=f"h_grp{g[0]}", align_bytes=64)
+            for n, c in enumerate(g):
+                layer1(c, h_grps[g], n * CH)
+
+        def h_quant(g):
+            h_codes[g] = keep.tile([P, CH * len(g)], U32, name=f"h_codes{g[0]}", align_bytes=64)
+            h_scales[g] = keep.tile([P, CH * len(g)], U8, name=f"h_scales{g[0]}", align_bytes=64)
             nc.vector.quantize_mx(
-                out=h_codes[:, lo : lo + width].bitcast(FP8X4),
-                scales=h_scales[:, lo : lo + width],
-                in_=h_grp[:].rearrange("p n t -> p (n t)"),
+                out=h_codes[g][:].bitcast(FP8X4),
+                scales=h_scales[g][:],
+                in_=h_grps[g][:].rearrange("p n t -> p (n t)"),
             )
 
-        def layer2(b, acc, lo, hi, base):
-            while lo < hi:
-                e = max(k for k in range(E) if STARTS[k] <= lo)
-                end = min(hi, STARTS[e] + COUNTS[e])
-                w = max(k for k in (128, 256, 512) if k <= end - lo)
-                nc.tensor.matmul_mx(
-                    out=acc[:, lo - base : lo - base + w],
-                    lhsT=w2_codes[:, e, 256 * b : 256 * b + 256].bitcast(FP4X4),
-                    lhsT_scale=w2s[:, e, 128 * b : 128 * b + 128],
-                    rhs=h_codes[:, lo : lo + w].bitcast(FP8X4),
-                    rhs_scale=h_scales[:, lo : lo + w],
-                    start=True,
-                    stop=True,
-                )
-                lo += w
+        for g in groups[:6]:
+            h_make(g)
+        for g in groups[:3]:
+            h_quant(g)
+        for g in groups[6:]:
+            h_make(g)
+        for g in groups[3:]:
+            h_quant(g)
 
-        groups = [(0, 1), (2, 3), (4, 5), (6, 7), (8,), (9,), (10,), (11,)]
-        y0 = None
+        def layer2(b, g, yp):
+            e = chunks[g[0]][0]
+            k, at = g[0] // 4, g[0] % 4 * CH
+            nc.tensor.matmul_mx(
+                out=yp[k][:, at : at + CH * len(g)],
+                lhsT=w2_codes[:, e, 256 * b : 256 * b + 256].bitcast(FP4X4),
+                lhsT_scale=w2s[:, e, 128 * b : 128 * b + 128],
+                rhs=h_codes[g][:].bitcast(FP8X4),
+                rhs_scale=h_scales[g][:],
+                start=True,
+                stop=True,
+            )
+
+        y0 = [psum.tile([P, 512], F32, name=f"yp{k}", bufs=1) for k in range(3)]
         for g in groups:
-            width = CH * len(g)
-            h_grp = keep.tile([P, width, PACK], BF16, name=f"h_grp{g[0]}", align_bytes=64)
-            for n, c in enumerate(g):
-                layer1(c, h_grp, n * CH)
-            lo = g[0] * CH
-            h_quant(h_grp, lo, width)
-            base = lo // 512 * 512
-            if lo == 0:
-                y0 = psum.tile([P, 3, 512], F32, name="yp", bufs=1)
-            k = base // 512
-            layer2(0, y0[:, k, :], lo, lo + width, base)
-            if g == (10,):
-                nc.scalar.activation(ys[0][:, base : base + 384], y0[:, k, 0:384], COPY)
+            layer2(0, g, y0)
+            if g == (3,) or g == (2, 3):
+                nc.scalar.activation(ys[0][:, 0:512], y0[0][:], COPY)
+            elif g == (7,):
+                nc.scalar.activation(ys[0][:, 512:1024], y0[1][:], COPY)
+            elif g == (10,):
+                nc.scalar.activation(ys[0][:, 1024:1408], y0[2][:, 0:384], COPY)
             elif g == (11,):
-                nc.vector.tensor_copy(ys[0][:, base + 384 : base + 512], y0[:, k, 384:512])
-            elif lo + width == base + 512:
-                nc.scalar.activation(ys[0][:, base : base + 512], y0[:, k, :], COPY)
+                nc.vector.tensor_copy(ys[0][:, 1408:1536], y0[2][:, 384:512])
 
         for b in (1, 2):
-            yb = psum.tile([P, 3, 512], F32, name="yp", bufs=1)
+            yb = [psum.tile([P, 512], F32, name=f"yp{k}", bufs=1) for k in range(3)]
+            for g in groups:
+                layer2(b, g, yb)
             for k in range(3):
-                layer2(b, yb[:, k, :], 512 * k, 512 * k + 512, 512 * k)
-                nc.scalar.activation(ys[b][:, 512 * k : 512 * k + 512], yb[:, k, :], COPY)
+                nc.scalar.activation(ys[b][:, 512 * k : 512 * k + 512], yb[k][:], COPY)
 
         def mul(b, r, lo, hi):
             g = ring.tile([P, T], F32, name=f"m{r}", align_bytes=64)

@@ -60,13 +60,20 @@ def tile_moe_rag_mlp_relu_kernel(
         def load_x(c):
             nc.sync.dma_start(out=x_raw[c][:], in_=xT[:, c * XC : (c + 1) * XC].rearrange("(p j) w -> p j w", j=PACK))
 
+        def load_w1(i):
+            nc.sync.dma_start(
+                out=w1_raw[:, 2 * i : 2 * i + 2, :].bitcast(I32),
+                in_=w1_words[2 * i : 2 * i + 2, 0].rearrange("e p b -> p e b").bitcast(I32),
+            )
+
         for q in range(4):
             nc.scalar.dma_start(
                 out=w1s_raw[32 * q : 32 * q + 4].bitcast(I32),
                 in_=w1_scales[:, 0, 4 * q : 4 * q + 4, :].rearrange("e q n -> q e n").bitcast(I32),
             )
-        nc.sync.dma_start(out=w1_raw[:].bitcast(I32), in_=w1_words[:, 0].rearrange("e p b -> p e b").bitcast(I32))
+        load_w1(0)
         load_x(0)
+        load_w1(1)
         load_x(1)
         load_x(2)
         nc.sync.dma_start(offs_t[:], offs)
@@ -96,35 +103,43 @@ def tile_moe_rag_mlp_relu_kernel(
             else:
                 nc.vector.tensor_copy(o, i)
 
-        nc.vector.tensor_copy(
-            out=w1_codes[:].bitcast(U16).rearrange("p e (t m) -> p e t m", t=PACK),
-            in_=w1_raw[:].bitcast(U16).rearrange("p e (m t) -> p e t m", t=PACK),
-        )
-        nc.vector.tensor_copy(
-            out=w1s[:].rearrange("p e (t m) -> p e t m", t=PACK),
-            in_=w1s_raw[:].rearrange("p e (m t) -> p e t m", t=PACK),
-        )
+        def w1_permute(i):
+            es = slice(2 * i, 2 * i + 2)
+            nc.vector.tensor_copy(
+                out=w1_codes[:, es, :].bitcast(U16).rearrange("p e (t m) -> p e t m", t=PACK),
+                in_=w1_raw[:, es, :].bitcast(U16).rearrange("p e (m t) -> p e t m", t=PACK),
+            )
+            nc.vector.tensor_copy(
+                out=w1s[:, es, :].rearrange("p e (t m) -> p e t m", t=PACK),
+                in_=w1s_raw[:, es, :].rearrange("p e (m t) -> p e t m", t=PACK),
+            )
+
         interleave("S", 0, 0, XC)
-        interleave("S", 1, 0, XC)
+        w1_permute(0)
+        w1_permute(1)
         x_quant(0)
+        interleave("S", 1, 0, 160)
+        interleave("V", 1, 160, XC)
         interleave("V", 2, 0, 160)
-        interleave("S", 2, 160, XC)
         x_quant(1)
+        interleave("S", 2, 160, XC)
         x_quant(2)
 
         xg = []
         xgs = []
         for e in range(E):
-            cols = slice(STARTS[e] // 16, (STARTS[e] + COUNTS[e]) // 16)
             words = keep.tile([P, COUNTS[e]], U32, name=f"xg{e}", align_bytes=64)
             bytes_ = keep.tile([P, COUNTS[e]], U8, name=f"xgs{e}", align_bytes=64)
-            nc.vector.tensor_copy(words[:], x_codes[:].indirect(offs_t[:, cols]))
-            nc.vector.tensor_copy(bytes_[:], x_scales[:].indirect(offs_t[:, cols]))
+            step = 256 if e == 2 else COUNTS[e]
+            for lo in range(0, COUNTS[e], step):
+                cols = slice((STARTS[e] + lo) // 16, (STARTS[e] + lo + step) // 16)
+                nc.vector.tensor_copy(words[:, lo : lo + step], x_codes[:].indirect(offs_t[:, cols]))
+                nc.vector.tensor_copy(bytes_[:, lo : lo + step], x_scales[:].indirect(offs_t[:, cols]))
             xg.append(words)
             xgs.append(bytes_)
 
         chunks = [(e, s) for e in range(E) for s in range(0, COUNTS[e], CH)]
-        vector_chunks = (9, 11)
+        vector_chunks = (7, 9, 11)
 
         def layer1(c, h_grp, at):
             e, s = chunks[c]
@@ -167,9 +182,12 @@ def tile_moe_rag_mlp_relu_kernel(
             h_make(g)
         for g in groups[:3]:
             h_quant(g)
-        for g in groups[6:]:
+        for g in groups[6:8]:
             h_make(g)
-        for g in groups[3:]:
+        for g in groups[3:5]:
+            h_quant(g)
+        h_make(groups[8])
+        for g in groups[5:]:
             h_quant(g)
 
         def layer2(b, g, yp):
@@ -205,7 +223,7 @@ def tile_moe_rag_mlp_relu_kernel(
                 nc.scalar.activation(ys[b][:, 512 * k : 512 * k + 512], yb[k][:], COPY)
 
         def mul(b, r, lo, hi):
-            g = ring.tile([P, T], F32, name=f"m{r}", align_bytes=64)
+            g = ring.tile([P, T], F32, name=f"m{r}", bufs=4, align_bytes=64)
             pos = (pos1_t, pos2_t)[r]
             nc.vector.tensor_tensor(
                 g[:, lo:hi], ys[b][:].indirect(pos[:, lo // 16 : hi // 16]), gates[b][:, r, lo:hi], MULT
@@ -213,16 +231,19 @@ def tile_moe_rag_mlp_relu_kernel(
             return g
 
         def finish(b, m1, m2, lo, hi):
-            o = ring.tile([P, T], F32, name="o", align_bytes=64)
+            o = ring.tile([P, T], F32, name="o", bufs=5, align_bytes=64)
             nc.vector.tensor_tensor(o[:, lo:hi], m1[:, lo:hi], m2[:, lo:hi], ADD)
             nc.sync.dma_start(out=out[b * P : (b + 1) * P, lo:hi], in_=o[:, lo:hi])
 
-        parts = [(0, 0, T), (1, 0, T), (2, 0, 512), (2, 512, T)]
+        parts = [(0, 0, T), (1, 0, T), (2, 0, 384), (2, 384, 576), (2, 576, T)]
         pending = None
         for b, lo, hi in parts:
             m1 = mul(b, 0, lo, hi)
+            if pending is not None and hi < T or b < 2 and pending is not None:
+                finish(*pending)
+                pending = None
+            m2 = mul(b, 1, lo, hi)
             if pending is not None:
                 finish(*pending)
-            m2 = mul(b, 1, lo, hi)
             pending = (b, m1, m2, lo, hi)
         finish(*pending)

@@ -53,9 +53,9 @@ def tile_moe_rag_mlp_relu_kernel(
         gates = [keep.tile([P, 2, T], F32, name=f"gates{b}", align_bytes=64) for b in range(3)]
         ys = [keep.tile([P, S], F32, name=f"y{b}", align_bytes=64) for b in range(3)]
 
-        nc.vector.memset(w1s_raw[:].rearrange("p e n -> p (e n)").bitcast(I32), 0)
-        nc.vector.memset(w2s[:].rearrange("p e n -> p (e n)").bitcast(I32), 0)
+        nc.gpsimd.memset(w1s_raw[:].rearrange("p e n -> p (e n)").bitcast(I32), 0)
         nc.gpsimd.memset(x_scales[:], 0)
+        nc.gpsimd.memset(w2s[:].rearrange("p e n -> p (e n)").bitcast(I32), 0)
 
         def load_x(c):
             nc.sync.dma_start(out=x_raw[c][:], in_=xT[:, c * XC : (c + 1) * XC].rearrange("(p j) w -> p j w", j=PACK))
@@ -96,8 +96,8 @@ def tile_moe_rag_mlp_relu_kernel(
             )
 
         def interleave(engine, c, lo, hi):
-            o = x_grp[c][:, lo:hi, :]
-            i = x_raw[c][:, :, lo:hi].rearrange("p j w -> p w j")
+            o = x_grp[c][:, lo:hi, :].rearrange("p (c i) t -> p c t i", i=4)
+            i = x_raw[c][:, :, lo:hi].rearrange("p t (c i) -> p c t i", i=4)
             if engine == "S":
                 nc.scalar.activation(o, i, COPY)
             else:

from contextlib import ExitStack

import concourse.mybir as mybir

K, T, E, H, N = 512, 768, 4, 512, 384
COUNTS = (256, 384, 512, 384)
STARTS = (0, 256, 640, 1152)
S = 1536
P = 128
PACK = 4
CH = 128
XC = 256
FLOPS = 2 * S * (K * H + H * N)

F32 = mybir.dt.float32
BF16 = mybir.dt.bfloat16
I32 = mybir.dt.int32
U32 = mybir.dt.uint32
U16 = mybir.dt.uint16
U8 = mybir.dt.uint8
FP8X4 = mybir.dt.float8_e4m3fn_x4
FP4X4 = mybir.dt.float4_e2m1fn_x4
COPY = mybir.ActivationFunctionType.Copy
RELU = mybir.ActivationFunctionType.Relu
MULT = mybir.AluOpType.mult
ADD = mybir.AluOpType.add


def tile_moe_rag_mlp_relu_kernel(
    tc, xT, w1_words, w1_scales, w2_words, w2_scales, gate, offs, pos1, pos2, out
):
    nc = tc.nc
    with ExitStack() as ctx:
        lists = ctx.enter_context(tc.tile_pool(name="lists", bufs=1))
        keep = ctx.enter_context(tc.tile_pool(name="keep", bufs=1))
        ring = ctx.enter_context(tc.tile_pool(name="ring", bufs=3))
        psum = ctx.enter_context(tc.psum_pool(name="psum", bufs=1))

        offs_t = lists.tile([P, 2 * T // 16], U16, name="offs_t")
        pos1_t = lists.tile([P, T // 16], U16, name="pos1_t")
        pos2_t = lists.tile([P, T // 16], U16, name="pos2_t")

        w1_raw = keep.tile([P, E, 2 * H], U8, name="w1_raw", align_bytes=64)
        w1_codes = keep.tile([P, E, 2 * H], U8, name="w1_codes", align_bytes=64)
        w1s_raw = keep.tile([P, E, H], U8, name="w1s_raw", align_bytes=64)
        w1s = keep.tile([P, E, H], U8, name="w1s", align_bytes=64)
        w2_codes = keep.tile([P, E, 2 * N], U8, name="w2_codes", align_bytes=64)
        w2s = keep.tile([P, E, N], U8, name="w2s", align_bytes=64)
        x_raw = [keep.tile([P, PACK, XC], F32, name=f"x_raw{c}", align_bytes=64) for c in range(3)]
        x_grp = [keep.tile([P, XC, PACK], BF16, name=f"x_grp{c}", align_bytes=64) for c in range(3)]
        x_codes = keep.tile([P, T], U32, name="x_codes", align_bytes=64)
        x_scales = keep.tile([P, T], U8, name="x_scales", align_bytes=64)
        gates = [keep.tile([P, 2, T], F32, name=f"gates{b}", align_bytes=64) for b in range(3)]
        ys = [keep.tile([P, S], F32, name=f"y{b}", align_bytes=64) for b in range(3)]

        nc.gpsimd.memset(w1s_raw[:].rearrange("p e n -> p (e n)").bitcast(I32), 0)
        nc.gpsimd.memset(x_scales[:], 0)
        nc.gpsimd.memset(w2s[:].rearrange("p e n -> p (e n)").bitcast(I32), 0)

        def load_x(c):
            nc.sync.dma_start(out=x_raw[c][:], in_=xT[:, c * XC : (c + 1) * XC].rearrange("(p j) w -> p j w", j=PACK))

        def load_w1(i):
            nc.sync.dma_start(
                out=w1_raw[:, 2 * i : 2 * i + 2, :].bitcast(I32),
                in_=w1_words[2 * i : 2 * i + 2, 0].rearrange("e p b -> p e b").bitcast(I32),
            )

        for q in range(4):
            nc.scalar.dma_start(
                out=w1s_raw[32 * q : 32 * q + 4].bitcast(I32),
                in_=w1_scales[:, 0, 4 * q : 4 * q + 4, :].rearrange("e q n -> q e n").bitcast(I32),
            )
        load_w1(0)
        load_x(0)
        load_w1(1)
        load_x(1)
        load_x(2)
        nc.sync.dma_start(offs_t[:], offs)
        nc.sync.dma_start(out=w2_codes[:].bitcast(I32), in_=w2_words[:, 0].rearrange("e p b -> p e b").bitcast(I32))
        for q in range(4):
            nc.sync.dma_start(
                out=w2s[32 * q : 32 * q + 4].bitcast(I32),
                in_=w2_scales[:, 0, 4 * q : 4 * q + 4, :].rearrange("e q n -> q e n").bitcast(I32),
            )
        nc.sync.dma_start(pos1_t[:], pos1)
        nc.sync.dma_start(pos2_t[:], pos2)
        for b in range(3):
            nc.sync.dma_start(out=gates[b][:], in_=gate[:, b * P : (b + 1) * P, :].rearrange("g p t -> p g t"))

        def x_quant(c):
            nc.vector.quantize_mx(
                out=x_codes[:, c * XC : (c + 1) * XC].bitcast(FP8X4),
                scales=x_scales[:, c * XC : (c + 1) * XC],
                in_=x_grp[c][:].rearrange("p w j -> p (w j)"),
            )

        def interleave(engine, c, lo, hi):
            o = x_grp[c][:, lo:hi, :].rearrange("p (c i) t -> p c t i", i=4)
            i = x_raw[c][:, :, lo:hi].rearrange("p t (c i) -> p c t i", i=4)
            if engine == "S":
                nc.scalar.activation(o, i, COPY)
            else:
                nc.vector.tensor_copy(o, i)

        def w1_permute(i):
            es = slice(2 * i, 2 * i + 2)
            nc.vector.tensor_copy(
                out=w1_codes[:, es, :].bitcast(U16).rearrange("p e (t m) -> p e t m", t=PACK),
                in_=w1_raw[:, es, :].bitcast(U16).rearrange("p e (m t) -> p e t m", t=PACK),
            )
            nc.vector.tensor_copy(
                out=w1s[:, es, :].rearrange("p e (t m) -> p e t m", t=PACK),
                in_=w1s_raw[:, es, :].rearrange("p e (m t) -> p e t m", t=PACK),
            )

        interleave("S", 0, 0, XC)
        w1_permute(0)
        w1_permute(1)
        x_quant(0)
        interleave("S", 1, 0, 160)
        interleave("V", 1, 160, XC)
        interleave("V", 2, 0, 160)
        x_quant(1)
        interleave("S", 2, 160, XC)
        x_quant(2)

        xg = []
        xgs = []
        for e in range(E):
            words = keep.tile([P, COUNTS[e]], U32, name=f"xg{e}", align_bytes=64)
            bytes_ = keep.tile([P, COUNTS[e]], U8, name=f"xgs{e}", align_bytes=64)
            step = 256 if e == 2 else COUNTS[e]
            for lo in range(0, COUNTS[e], step):
                cols = slice((STARTS[e] + lo) // 16, (STARTS[e] + lo + step) // 16)
                nc.vector.tensor_copy(words[:, lo : lo + step], x_codes[:].indirect(offs_t[:, cols]))
                nc.vector.tensor_copy(bytes_[:, lo : lo + step], x_scales[:].indirect(offs_t[:, cols]))
            xg.append(words)
            xgs.append(bytes_)

        chunks = [(e, s) for e in range(E) for s in range(0, COUNTS[e], CH)]
        vector_chunks = (7, 9, 11)

        def layer1(c, h_grp, at):
            e, s = chunks[c]
            acc = psum.tile([P, PACK, CH], F32, name="acc", bufs=5)
            for t in range(PACK):
                nc.tensor.matmul_mx(
                    out=acc[:, t, :],
                    lhsT=w1_codes[:, e, 256 * t : 256 * t + 256].bitcast(FP4X4),
                    lhsT_scale=w1s[:, e, 128 * t : 128 * t + 128],
                    rhs=xg[e][:, s : s + CH].bitcast(FP8X4),
                    rhs_scale=xgs[e][:, s : s + CH],
                    start=True,
                    stop=True,
                )
            o = h_grp[:, at : at + CH, :]
            a = acc[:].rearrange("p t n -> p n t")
            if c in vector_chunks:
                nc.vector.tensor_scalar_max(o, a, 0.0)
            else:
                nc.scalar.activation(o, a, RELU)

        groups = [(0, 1), (2, 3), (4,), (5, 6), (7,), (8,), (9,), (10,), (11,)]
        h_grps, h_codes, h_scales = {}, {}, {}

        def h_make(g):
            h_grps[g] = keep.tile([P, CH * len(g), PACK], BF16, name=f"h_grp{g[0]}", align_bytes=64)
            for n, c in enumerate(g):
                layer1(c, h_grps[g], n * CH)

        def h_quant(g):
            h_codes[g] = keep.tile([P, CH * len(g)], U32, name=f"h_codes{g[0]}", align_bytes=64)
            h_scales[g] = keep.tile([P, CH * len(g)], U8, name=f"h_scales{g[0]}", align_bytes=64)
            nc.vector.quantize_mx(
                out=h_codes[g][:].bitcast(FP8X4),
                scales=h_scales[g][:],
                in_=h_grps[g][:].rearrange("p n t -> p (n t)"),
            )

        for g in groups[:6]:
            h_make(g)
        for g in groups[:3]:
            h_quant(g)
        for g in groups[6:8]:
            h_make(g)
        for g in groups[3:5]:
            h_quant(g)
        h_make(groups[8])
        for g in groups[5:]:
            h_quant(g)

        def layer2(b, g, yp):
            e = chunks[g[0]][0]
            k, at = g[0] // 4, g[0] % 4 * CH
            nc.tensor.matmul_mx(
                out=yp[k][:, at : at + CH * len(g)],
                lhsT=w2_codes[:, e, 256 * b : 256 * b + 256].bitcast(FP4X4),
                lhsT_scale=w2s[:, e, 128 * b : 128 * b + 128],
                rhs=h_codes[g][:].bitcast(FP8X4),
                rhs_scale=h_scales[g][:],
                start=True,
                stop=True,
            )

        y0 = [psum.tile([P, 512], F32, name=f"yp{k}", bufs=1) for k in range(3)]
        for g in groups:
            layer2(0, g, y0)
            if g == (3,) or g == (2, 3):
                nc.scalar.activation(ys[0][:, 0:512], y0[0][:], COPY)
            elif g == (7,):
                nc.scalar.activation(ys[0][:, 512:1024], y0[1][:], COPY)
            elif g == (10,):
                nc.scalar.activation(ys[0][:, 1024:1408], y0[2][:, 0:384], COPY)
            elif g == (11,):
                nc.vector.tensor_copy(ys[0][:, 1408:1536], y0[2][:, 384:512])

        for b in (1, 2):
            yb = [psum.tile([P, 512], F32, name=f"yp{k}", bufs=1) for k in range(3)]
            for g in groups:
                layer2(b, g, yb)
            for k in range(3):
                nc.scalar.activation(ys[b][:, 512 * k : 512 * k + 512], yb[k][:], COPY)

        def mul(b, r, lo, hi):
            g = ring.tile([P, T], F32, name=f"m{r}", bufs=4, align_bytes=64)
            pos = (pos1_t, pos2_t)[r]
            nc.vector.tensor_tensor(
                g[:, lo:hi], ys[b][:].indirect(pos[:, lo // 16 : hi // 16]), gates[b][:, r, lo:hi], MULT
            )
            return g

        def finish(b, m1, m2, lo, hi):
            o = ring.tile([P, T], F32, name="o", bufs=5, align_bytes=64)
            nc.vector.tensor_tensor(o[:, lo:hi], m1[:, lo:hi], m2[:, lo:hi], ADD)
            nc.sync.dma_start(out=out[b * P : (b + 1) * P, lo:hi], in_=o[:, lo:hi])

        parts = [(0, 0, T), (1, 0, T), (2, 0, 384), (2, 384, 576), (2, 576, T)]
        pending = None
        for b, lo, hi in parts:
            m1 = mul(b, 0, lo, hi)
            if pending is not None and hi < T or b < 2 and pending is not None:
                finish(*pending)
                pending = None
            m2 = mul(b, 1, lo, hi)
            if pending is not None:
                finish(*pending)
            pending = (b, m1, m2, lo, hi)
        finish(*pending)
